import numpy as np, ml_dtypes
CORES = [24,25,26,27,28,29,30,31,224,225,226,227,228,229,230,231]
N = 16
C = 128
def setup_inputs(rng):
    x = 150 * rng.standard_normal((1, 128, C), dtype=np.float32) + 2 * rng.standard_normal((N, 128, C), dtype=np.float32)
    x = (x + rng.uniform(100, 300, (1, 128, C)) * (rng.random((1, 128, C)) < 0.7) * (rng.random((N, 128, C)) < 0.5)).astype(np.float32)
    return {"x": x}
def setup_inputs_trail(rng):
    d = setup_inputs(rng); x = d["x"].copy(); t = int(rng.integers(N))
    x[t] = np.delete(x, t, axis=0).max(axis=0) - rng.uniform(3.0, 20.0, x[t].shape).astype(np.float32)
    return {"x": x}
def reference(x):
    X = x.astype(np.float64)
    P = np.exp(X - X.max(axis=0))
    return {"y": (P / P.sum(axis=0)).astype(ml_dtypes.bfloat16)}

@@ -1,0 +1,161 @@
+from concourse.bass import DstId, RemoteDMATransfer
+from concourse.mybir import AluOpType, ActivationFunctionType
+
+P, C = 128, 128
+CLAMP = 60.0
+
+SCRATCH = {
+    "xs": ("sbuf", [P, C], "float32"),
+    "land": ("sbuf", [P, 2 * C], "float32"),
+    "t1": ("sbuf", [P, C], "float32"),
+    "t2": ("sbuf", [P, C // 2], "float32"),
+    "p": ("sbuf", [P, 2 * C], "float32"),
+    "ms": ("sbuf", [P, C // 2], "bfloat16"),
+    "msr": ("sbuf", [P, C // 2], "bfloat16"),
+    "ma": ("sbuf", [P, C // 4], "float32"),
+    "d": ("sbuf", [P, C // 4], "float32"),
+    "e": ("sbuf", [P, C // 4], "float32"),
+    "r": ("sbuf", [P, C // 4], "float32"),
+    "yb": ("sbuf", [P, 2 * C], "bfloat16"),
+    "yl": ("sbuf", [P, C], "bfloat16"),
+}
+SEMAPHORES = ["ld", "sent", "arr1", "arr2", "arr3", "st"] + ["c%d" % i for i in range(1, 18)]
+
+
+def _engines(mask):
+    return [b for b in range(mask.bit_length()) if (mask >> b) & 1]
+
+
+def _shares(n, d):
+    s = 1
+    while 2 * s * d <= n:
+        s *= 2
+    out = [s] * d
+    left = n - s * d
+    for i in range(d):
+        if out[i] <= left:
+            left -= out[i]
+            out[i] *= 2
+    return out
+
+
+def _fan(topo, src, dsts):
+    m = topo.mask(src, dsts[0])
+    for t in dsts:
+        m &= topo.mask(src, t)
+    eng = _engines(m)
+    res, at = {}, 0
+    for t, n in zip(dsts, _shares(len(eng), len(dsts))):
+        res[t] = (sum(1 << b for b in eng[at:at + n]), n)
+        at += n
+    return res
+
+
+def rank_program(g, core, T, topo):
+    if T.rank_of(core) is None:
+        return
+    V, S, Y, sem, A = g.vector, g.scalar, g.sync, T.sem, AluOpType
+    Exp = ActivationFunctionType.Exp
+
+    def chip_of(c):
+        return (topo.host(c), topo.chip(c))
+
+    here = [c for c in T.cores if chip_of(c) == chip_of(core)]
+    there = [c for c in T.cores if chip_of(c) != chip_of(core)]
+
+    def gates(a, b):
+        return sorted([c for c in a if all(topo.may_write(c, t) for t in b)], key=lambda c: (topo.die(c), c))
+
+    own, far = gates(here, there), gates(there, here)
+    K, R = len(own), len(here)
+    W = C // K
+    j = here.index(core)
+
+    def blk(t, i):
+        return t[:, i * W:(i + 1) * W]
+
+    def dst(t):
+        rid, pid = topo.addr(t, core)
+        return DstId(rid=rid, pnc=pid)
+
+    scatter = {c: _fan(topo, c, [o for o in own if o != c]) for c in here}
+    gather = {o: _fan(topo, o, [c for c in here if c != o]) for o in own}
+    sent = 0
+
+    Y.dma_start(T.xs[:], T.x[:]).then_inc(sem.ld, 16)
+    if core in own:
+        k = own.index(core)
+        S.dma_start(blk(T.land, j), blk(T.x, k)).then_inc(sem.arr1, 16)
+
+    g.wait_ge(sem.ld, 16)
+    g.remote_dma_fused(
+        [RemoteDMATransfer(dst_ids=[dst(o)], dma_engine_mask=m, remote_sem=sem.arr1,
+                           src=blk(T.xs, own.index(o)), dst=blk(T.land, j))
+         for o, (m, n) in scatter[core].items()], local_sem=sem.sent)
+    sent += sum(n for m, n in scatter[core].values())
+
+    if core in own:
+        k = own.index(core)
+        H = R * W // 2
+        m_a, s_a = T.ms[:, 0:W], T.ms[:, W:2 * W]
+        m_b, s_b = T.msr[:, 0:W], T.msr[:, W:2 * W]
+        V.wait_ge(sem.arr1, 16 + sum(scatter[c][core][1] for c in here if c != core))
+        V.tensor_tensor(T.t1[:, 0:H], T.land[:, 0:H], T.land[:, H:2 * H], A.max).then_inc(sem.c1, 1)
+        V.wait_ge(sem.c1, 1)
+        V.tensor_tensor(T.t2[:, 0:H // 2], T.t1[:, 0:H // 2], T.t1[:, H // 2:H], A.max).then_inc(sem.c2, 1)
+        V.wait_ge(sem.c2, 1)
+        V.tensor_tensor(m_a, T.t2[:, 0:W], T.t2[:, W:2 * W], A.max).then_inc(sem.c3, 1)
+        V.wait_ge(sem.c3, 1)
+        V.tensor_tensor(blk(T.p, 0), blk(T.land, 0), m_a, A.subtract).then_inc(sem.c4, 1)
+        for i in range(1, R):
+            V.tensor_tensor(blk(T.p, i), blk(T.land, i), m_a, A.subtract).then_inc(sem.c5, 1)
+        S.wait_ge(sem.c4, 1)
+        S.activation(blk(T.p, 0), blk(T.p, 0), Exp).then_inc(sem.c6, 1)
+        S.wait_ge(sem.c5, R - 1)
+        S.activation(T.p[:, W:R * W], T.p[:, W:R * W], Exp).then_inc(sem.c6, 1)
+        V.wait_ge(sem.c6, 2)
+        V.tensor_tensor(T.t1[:, 0:H], T.p[:, 0:H], T.p[:, H:2 * H], A.add).then_inc(sem.c7, 1)
+        V.wait_ge(sem.c7, 1)
+        V.tensor_tensor(T.t2[:, 0:H // 2], T.t1[:, 0:H // 2], T.t1[:, H // 2:H], A.add).then_inc(sem.c8, 1)
+        V.wait_ge(sem.c8, 1)
+        V.tensor_tensor(s_a, T.t2[:, 0:W], T.t2[:, W:2 * W], A.add).then_inc(sem.c9, 1)
+
+        partner = far[k]
+        rid, pid = topo.addr(partner, core)
+        mk = topo.mask(core, partner)
+        g.wait_ge(sem.c9, 1)
+        g.remote_dma(T.msr[:], T.ms[:], sem.arr2, sem.sent, pid, rid, mk)
+        sent += len(_engines(mk))
+
+        V.tensor_scalar(T.ma[:], m_a, CLAMP, None, A.add).then_inc(sem.c10, 1)
+        V.wait_ge(sem.c10, 1)
+        V.wait_ge(sem.c9, 1)
+        V.wait_ge(sem.arr2, len(_engines(topo.mask(partner, core))))
+        V.tensor_tensor(T.d[:], m_b, T.ma[:], A.min).then_inc(sem.c11, 1)
+        V.wait_ge(sem.c11, 1)
+        V.tensor_tensor(T.d[:], T.d[:], m_a, A.subtract).then_inc(sem.c12, 1)
+        S.wait_ge(sem.c12, 1)
+        S.activation(T.e[:], T.d[:], Exp).then_inc(sem.c13, 1)
+        V.wait_ge(sem.c13, 1)
+        V.tensor_tensor(T.e[:], T.e[:], s_b, A.mult).then_inc(sem.c14, 1)
+        V.wait_ge(sem.c14, 1)
+        V.tensor_tensor(T.e[:], T.e[:], s_a, A.add).then_inc(sem.c15, 1)
+        V.wait_ge(sem.c15, 1)
+        V.reciprocal(T.r[:], T.e[:]).then_inc(sem.c16, 1)
+        V.wait_ge(sem.c16, 1)
+        for i in range(R):
+            if i != j:
+                V.tensor_tensor(blk(T.yb, i), blk(T.p, i), T.r[:], A.mult).then_inc(sem.c17, 1)
+        V.tensor_tensor(blk(T.yl, k), blk(T.p, j), T.r[:], A.mult).then_inc(sem.arr3, 1)
+
+        g.wait_ge(sem.c17, R - 1)
+        g.remote_dma_fused(
+            [RemoteDMATransfer(dst_ids=[dst(c)], dma_engine_mask=m, remote_sem=sem.arr3,
+                               src=blk(T.yb, here.index(c)), dst=blk(T.yl, k))
+             for c, (m, n) in gather[core].items()], local_sem=sem.sent)
+        sent += sum(n for m, n in gather[core].values())
+
+    Y.wait_ge(sem.arr3, sum(gather[o][core][1] for o in own if o != core) + (1 if core in own else 0))
+    Y.dma_start(T.y[:], T.yl[:]).then_inc(sem.st, 16)
+    g.wait_ge(sem.sent, sent)
+    g.wait_ge(sem.st, 16)

@@ -3,13 +3,19 @@ from concourse.mybir import AluOpType, ActivationFunctionType
 
 P, C = 128, 128
 CLAMP = 60.0
+BANK = 512
 
 SCRATCH = {
     "xs": ("sbuf", [P, C], "float32"),
     "land": ("sbuf", [P, 2 * C], "float32"),
-    "t1": ("sbuf", [P, C], "float32"),
+    "h": ("sbuf", [P, C // 4], "bfloat16"),
+    "q": ("sbuf", [P, C // 4], "float32"),
+    "ta": ("sbuf", [P, C // 2], "float32"),
     "t2": ("sbuf", [P, C // 2], "float32"),
-    "p": ("sbuf", [P, 2 * C], "float32"),
+    "tb": ("psum", [P, BANK], "float32"),
+    "z": ("sbuf", [P, 2 * C], "float32"),
+    "pa": ("psum", [P, BANK], "float32"),
+    "pb": ("psum", [P, BANK], "float32"),
     "ms": ("sbuf", [P, C // 2], "bfloat16"),
     "msr": ("sbuf", [P, C // 2], "bfloat16"),
     "ma": ("sbuf", [P, C // 4], "float32"),
@@ -19,7 +25,8 @@ SCRATCH = {
     "yb": ("sbuf", [P, 2 * C], "bfloat16"),
     "yl": ("sbuf", [P, C], "bfloat16"),
 }
-SEMAPHORES = ["ld", "sent", "arr1", "arr2", "arr3", "st"] + ["c%d" % i for i in range(1, 18)]
+SEMAPHORES = ["ld", "ob", "sent", "arr1", "arr2", "arr3", "st", "sub1", "sub2", "sub3", "out"] + \
+             ["c%d" % i for i in range(1, 25)]
 
 
 def _engines(mask):
@@ -69,10 +76,12 @@ def rank_program(g, core, T, topo):
     own, far = gates(here, there), gates(there, here)
     K, R = len(own), len(here)
     W = C // K
-    j = here.index(core)
 
-    def blk(t, i):
-        return t[:, i * W:(i + 1) * W]
+    def blk(t, i, n=1):
+        return t[:, i * W:(i + n) * W]
+
+    def slot(o, c):
+        return 0 if c == o else 1 + [x for x in here if x != o].index(c)
 
     def dst(t):
         rid, pid = topo.addr(t, core)
@@ -81,77 +90,104 @@ def rank_program(g, core, T, topo):
     scatter = {c: _fan(topo, c, [o for o in own if o != c]) for c in here}
     gather = {o: _fan(topo, o, [c for c in here if c != o]) for o in own}
     sent = 0
+    count = [0]
+
+    def done(instr):
+        count[0] += 1
+        s = sem["c%d" % count[0]]
+        instr.then_inc(s, 1)
+        return s
 
     Y.dma_start(T.xs[:], T.x[:]).then_inc(sem.ld, 16)
     if core in own:
-        k = own.index(core)
-        S.dma_start(blk(T.land, j), blk(T.x, k)).then_inc(sem.arr1, 16)
+        S.dma_start(blk(T.land, 0), blk(T.x, own.index(core))).then_inc(sem.ob, 16)
 
     g.wait_ge(sem.ld, 16)
     g.remote_dma_fused(
         [RemoteDMATransfer(dst_ids=[dst(o)], dma_engine_mask=m, remote_sem=sem.arr1,
-                           src=blk(T.xs, own.index(o)), dst=blk(T.land, j))
+                           src=blk(T.xs, own.index(o)), dst=blk(T.land, slot(o, core)))
          for o, (m, n) in scatter[core].items()], local_sem=sem.sent)
     sent += sum(n for m, n in scatter[core].values())
 
     if core in own:
         k = own.index(core)
-        H = R * W // 2
-        m_a, s_a = T.ms[:, 0:W], T.ms[:, W:2 * W]
-        m_b, s_b = T.msr[:, 0:W], T.msr[:, W:2 * W]
-        V.wait_ge(sem.arr1, 16 + sum(scatter[c][core][1] for c in here if c != core))
-        V.tensor_tensor(T.t1[:, 0:H], T.land[:, 0:H], T.land[:, H:2 * H], A.max).then_inc(sem.c1, 1)
-        V.wait_ge(sem.c1, 1)
-        V.tensor_tensor(T.t2[:, 0:H // 2], T.t1[:, 0:H // 2], T.t1[:, H // 2:H], A.max).then_inc(sem.c2, 1)
-        V.wait_ge(sem.c2, 1)
-        V.tensor_tensor(m_a, T.t2[:, 0:W], T.t2[:, W:2 * W], A.max).then_inc(sem.c3, 1)
-        V.wait_ge(sem.c3, 1)
-        V.tensor_tensor(blk(T.p, 0), blk(T.land, 0), m_a, A.subtract).then_inc(sem.c4, 1)
+        m_a, s_a = blk(T.ms, 0), blk(T.ms, 1)
+        m_b, s_b = blk(T.msr, 0), blk(T.msr, 1)
+
+        def p(i):
+            return blk(T.z, i) if i < 4 else blk(T.pa, i - 4) if i < 6 else blk(T.pb, i - 6)
+
+        V.wait_ge(sem.ob, 16)
+        s = done(V.tensor_copy(T.h[:], blk(T.land, 0)))
+        V.wait_ge(s, 1)
+        s = done(V.tensor_tensor(T.q[:], blk(T.land, 0), T.h[:], A.subtract))
+        S.wait_ge(s, 1)
+        sq = done(S.activation(T.q[:], T.q[:], Exp))
+
+        V.wait_ge(sem.arr1, sum(scatter[c][core][1] for c in here if c != core))
+        s1 = done(V.tensor_tensor(T.ta[:], blk(T.land, 0, 2), blk(T.land, 4, 2), A.max))
+        s2 = done(V.tensor_tensor(blk(T.tb, 0, 2), blk(T.land, 2, 2), blk(T.land, 6, 2), A.max))
+        V.wait_ge(s1, 1)
+        V.wait_ge(s2, 1)
+        s = done(V.tensor_tensor(T.t2[:], T.ta[:], blk(T.tb, 0, 2), A.max))
+        V.wait_ge(s, 1)
+        s = done(V.tensor_tensor(m_a, blk(T.t2, 0), blk(T.t2, 1), A.max))
+        V.wait_ge(s, 1)
+        V.tensor_tensor(blk(T.z, 0), T.h[:], m_a, A.subtract).then_inc(sem.sub1, 1)
         for i in range(1, R):
-            V.tensor_tensor(blk(T.p, i), blk(T.land, i), m_a, A.subtract).then_inc(sem.c5, 1)
-        S.wait_ge(sem.c4, 1)
-        S.activation(blk(T.p, 0), blk(T.p, 0), Exp).then_inc(sem.c6, 1)
-        S.wait_ge(sem.c5, R - 1)
-        S.activation(T.p[:, W:R * W], T.p[:, W:R * W], Exp).then_inc(sem.c6, 1)
-        V.wait_ge(sem.c6, 2)
-        V.tensor_tensor(T.t1[:, 0:H], T.p[:, 0:H], T.p[:, H:2 * H], A.add).then_inc(sem.c7, 1)
-        V.wait_ge(sem.c7, 1)
-        V.tensor_tensor(T.t2[:, 0:H // 2], T.t1[:, 0:H // 2], T.t1[:, H // 2:H], A.add).then_inc(sem.c8, 1)
-        V.wait_ge(sem.c8, 1)
-        V.tensor_tensor(s_a, T.t2[:, 0:W], T.t2[:, W:2 * W], A.add).then_inc(sem.c9, 1)
+            V.tensor_tensor(blk(T.z, i), blk(T.land, i), m_a, A.subtract).then_inc(
+                sem.sub1 if i < 4 else sem.sub2 if i < 6 else sem.sub3, 1)
+        S.wait_ge(sem.sub1, 4)
+        e1 = done(S.activation(blk(T.z, 0, 4), blk(T.z, 0, 4), Exp))
+        S.wait_ge(sem.sub2, 2)
+        e2 = done(S.activation(blk(T.pa, 0, 2), blk(T.z, 4, 2), Exp))
+        S.wait_ge(sem.sub3, 2)
+        e3 = done(S.activation(blk(T.pb, 0, 2), blk(T.z, 6, 2), Exp))
+        V.wait_ge(sq, 1)
+        V.wait_ge(e1, 1)
+        s = done(V.tensor_tensor(blk(T.z, 0), blk(T.z, 0), T.q[:], A.mult))
+        V.wait_ge(s, 1)
+        V.wait_ge(e2, 1)
+        s1 = done(V.tensor_tensor(T.ta[:], blk(T.z, 0, 2), blk(T.pa, 0, 2), A.add))
+        V.wait_ge(e3, 1)
+        s2 = done(V.tensor_tensor(blk(T.tb, 2, 2), blk(T.z, 2, 2), blk(T.pb, 0, 2), A.add))
+        V.wait_ge(s1, 1)
+        V.wait_ge(s2, 1)
+        s = done(V.tensor_tensor(T.t2[:], T.ta[:], blk(T.tb, 2, 2), A.add))
+        V.wait_ge(s, 1)
+        ss = done(V.tensor_tensor(s_a, blk(T.t2, 0), blk(T.t2, 1), A.add))
 
         partner = far[k]
         rid, pid = topo.addr(partner, core)
         mk = topo.mask(core, partner)
-        g.wait_ge(sem.c9, 1)
+        g.wait_ge(ss, 1)
         g.remote_dma(T.msr[:], T.ms[:], sem.arr2, sem.sent, pid, rid, mk)
         sent += len(_engines(mk))
 
-        V.tensor_scalar(T.ma[:], m_a, CLAMP, None, A.add).then_inc(sem.c10, 1)
-        V.wait_ge(sem.c10, 1)
-        V.wait_ge(sem.c9, 1)
+        s = done(V.tensor_scalar(T.ma[:], m_a, CLAMP, None, A.add))
+        V.wait_ge(s, 1)
+        V.wait_ge(ss, 1)
         V.wait_ge(sem.arr2, len(_engines(topo.mask(partner, core))))
-        V.tensor_tensor(T.d[:], m_b, T.ma[:], A.min).then_inc(sem.c11, 1)
-        V.wait_ge(sem.c11, 1)
-        V.tensor_tensor(T.d[:], T.d[:], m_a, A.subtract).then_inc(sem.c12, 1)
-        S.wait_ge(sem.c12, 1)
-        S.activation(T.e[:], T.d[:], Exp).then_inc(sem.c13, 1)
-        V.wait_ge(sem.c13, 1)
-        V.tensor_tensor(T.e[:], T.e[:], s_b, A.mult).then_inc(sem.c14, 1)
-        V.wait_ge(sem.c14, 1)
-        V.tensor_tensor(T.e[:], T.e[:], s_a, A.add).then_inc(sem.c15, 1)
-        V.wait_ge(sem.c15, 1)
-        V.reciprocal(T.r[:], T.e[:]).then_inc(sem.c16, 1)
-        V.wait_ge(sem.c16, 1)
-        for i in range(R):
-            if i != j:
-                V.tensor_tensor(blk(T.yb, i), blk(T.p, i), T.r[:], A.mult).then_inc(sem.c17, 1)
-        V.tensor_tensor(blk(T.yl, k), blk(T.p, j), T.r[:], A.mult).then_inc(sem.arr3, 1)
+        s = done(V.tensor_tensor(T.d[:], m_b, T.ma[:], A.min))
+        V.wait_ge(s, 1)
+        s = done(V.tensor_tensor(T.d[:], T.d[:], m_a, A.subtract))
+        S.wait_ge(s, 1)
+        s = done(S.activation(T.e[:], T.d[:], Exp))
+        V.wait_ge(s, 1)
+        s = done(V.tensor_tensor(T.e[:], T.e[:], s_b, A.mult))
+        V.wait_ge(s, 1)
+        s = done(V.tensor_tensor(T.e[:], T.e[:], s_a, A.add))
+        V.wait_ge(s, 1)
+        s = done(V.reciprocal(T.r[:], T.e[:]))
+        V.wait_ge(s, 1)
+        for i in range(1, R):
+            V.tensor_tensor(blk(T.yb, i), p(i), T.r[:], A.mult).then_inc(sem.out, 1)
+        V.tensor_tensor(blk(T.yl, k), p(0), T.r[:], A.mult).then_inc(sem.arr3, 1)
 
-        g.wait_ge(sem.c17, R - 1)
+        g.wait_ge(sem.out, R - 1)
         g.remote_dma_fused(
             [RemoteDMATransfer(dst_ids=[dst(c)], dma_engine_mask=m, remote_sem=sem.arr3,
-                               src=blk(T.yb, here.index(c)), dst=blk(T.yl, k))
+                               src=blk(T.yb, slot(core, c)), dst=blk(T.yl, k))
              for c, (m, n) in gather[core].items()], local_sem=sem.sent)
         sent += sum(n for m, n in gather[core].values())
 

@@ -16,17 +16,19 @@ SCRATCH = {
     "z": ("sbuf", [P, 2 * C], "float32"),
     "pa": ("psum", [P, BANK], "float32"),
     "pb": ("psum", [P, BANK], "float32"),
-    "ms": ("sbuf", [P, C // 2], "bfloat16"),
-    "msr": ("sbuf", [P, C // 2], "bfloat16"),
-    "ma": ("sbuf", [P, C // 4], "float32"),
+    "ma": ("sbuf", [P, C // 4], "bfloat16"),
+    "sa": ("sbuf", [P, C // 4], "bfloat16"),
+    "mb": ("sbuf", [P, C // 4], "bfloat16"),
+    "sb": ("sbuf", [P, C // 4], "bfloat16"),
     "d": ("sbuf", [P, C // 4], "float32"),
-    "e": ("sbuf", [P, C // 4], "float32"),
+    "f": ("sbuf", [P, C // 4], "float32"),
+    "c": ("sbuf", [P, C // 4], "float32"),
     "r": ("sbuf", [P, C // 4], "float32"),
     "yb": ("sbuf", [P, 2 * C], "bfloat16"),
     "yl": ("sbuf", [P, C], "bfloat16"),
 }
-SEMAPHORES = ["ld", "ob", "sent", "arr1", "arr2", "arr3", "st", "sub1", "sub2", "sub3", "out"] + \
-             ["c%d" % i for i in range(1, 25)]
+SEMAPHORES = ["ld", "ob", "sent", "arr1", "arrm", "arrs", "arr3", "st", "sub0", "sub1", "sub2", "sub3", "reb", "out"] + \
+             ["c%d" % i for i in range(1, 27)]
 
 
 def _engines(mask):
@@ -111,8 +113,10 @@ def rank_program(g, core, T, topo):
 
     if core in own:
         k = own.index(core)
-        m_a, s_a = blk(T.ms, 0), blk(T.ms, 1)
-        m_b, s_b = blk(T.msr, 0), blk(T.msr, 1)
+        partner = far[k]
+        rid, pid = topo.addr(partner, core)
+        mk = topo.mask(core, partner)
+        n_out, n_in = len(_engines(mk)), len(_engines(topo.mask(partner, core)))
 
         def p(i):
             return blk(T.z, i) if i < 4 else blk(T.pa, i - 4) if i < 6 else blk(T.pb, i - 6)
@@ -131,22 +135,30 @@ def rank_program(g, core, T, topo):
         V.wait_ge(s2, 1)
         s = done(V.tensor_tensor(T.t2[:], T.ta[:], blk(T.tb, 0, 2), A.max))
         V.wait_ge(s, 1)
-        s = done(V.tensor_tensor(m_a, blk(T.t2, 0), blk(T.t2, 1), A.max))
-        V.wait_ge(s, 1)
-        V.tensor_tensor(blk(T.z, 0), T.h[:], m_a, A.subtract).then_inc(sem.sub1, 1)
+        sm = done(V.tensor_tensor(T.ma[:], blk(T.t2, 0), blk(T.t2, 1), A.max))
+
+        g.wait_ge(sm, 1)
+        g.remote_dma(T.mb[:], T.ma[:], sem.arrm, sem.sent, pid, rid, mk)
+        sent += n_out
+
+        V.wait_ge(sm, 1)
+        V.tensor_tensor(blk(T.z, 0), T.h[:], T.ma[:], A.subtract).then_inc(sem.sub0, 1)
         for i in range(1, R):
-            V.tensor_tensor(blk(T.z, i), blk(T.land, i), m_a, A.subtract).then_inc(
+            V.tensor_tensor(blk(T.z, i), blk(T.land, i), T.ma[:], A.subtract).then_inc(
                 sem.sub1 if i < 4 else sem.sub2 if i < 6 else sem.sub3, 1)
-        S.wait_ge(sem.sub1, 4)
-        e1 = done(S.activation(blk(T.z, 0, 4), blk(T.z, 0, 4), Exp))
+        S.wait_ge(sem.sub0, 1)
+        e0 = done(S.activation(blk(T.z, 0), blk(T.z, 0), Exp))
+        S.wait_ge(sem.sub1, 3)
+        e1 = done(S.activation(blk(T.z, 1, 3), blk(T.z, 1, 3), Exp))
         S.wait_ge(sem.sub2, 2)
         e2 = done(S.activation(blk(T.pa, 0, 2), blk(T.z, 4, 2), Exp))
         S.wait_ge(sem.sub3, 2)
         e3 = done(S.activation(blk(T.pb, 0, 2), blk(T.z, 6, 2), Exp))
         V.wait_ge(sq, 1)
-        V.wait_ge(e1, 1)
+        V.wait_ge(e0, 1)
         s = done(V.tensor_tensor(blk(T.z, 0), blk(T.z, 0), T.q[:], A.mult))
         V.wait_ge(s, 1)
+        V.wait_ge(e1, 1)
         V.wait_ge(e2, 1)
         s1 = done(V.tensor_tensor(T.ta[:], blk(T.z, 0, 2), blk(T.pa, 0, 2), A.add))
         V.wait_ge(e3, 1)
@@ -155,30 +167,29 @@ def rank_program(g, core, T, topo):
         V.wait_ge(s2, 1)
         s = done(V.tensor_tensor(T.t2[:], T.ta[:], blk(T.tb, 2, 2), A.add))
         V.wait_ge(s, 1)
-        ss = done(V.tensor_tensor(s_a, blk(T.t2, 0), blk(T.t2, 1), A.add))
+        ss = done(V.tensor_tensor(T.sa[:], blk(T.t2, 0), blk(T.t2, 1), A.add))
 
-        partner = far[k]
-        rid, pid = topo.addr(partner, core)
-        mk = topo.mask(core, partner)
         g.wait_ge(ss, 1)
-        g.remote_dma(T.msr[:], T.ms[:], sem.arr2, sem.sent, pid, rid, mk)
-        sent += len(_engines(mk))
+        g.remote_dma(T.sb[:], T.sa[:], sem.arrs, sem.sent, pid, rid, mk)
+        sent += n_out
 
-        s = done(V.tensor_scalar(T.ma[:], m_a, CLAMP, None, A.add))
+        V.wait_ge(sem.arrm, n_in)
+        s = done(V.tensor_tensor(T.d[:], T.mb[:], T.ma[:], A.subtract))
+        V.wait_ge(s, 1)
+        s = done(V.tensor_scalar(T.d[:], T.d[:], CLAMP, -CLAMP, A.min, A.max))
+        S.wait_ge(s, 1)
+        s = done(S.activation(T.f[:], T.d[:], Exp, scale=-1.0))
         V.wait_ge(s, 1)
         V.wait_ge(ss, 1)
-        V.wait_ge(sem.arr2, len(_engines(topo.mask(partner, core))))
-        s = done(V.tensor_tensor(T.d[:], m_b, T.ma[:], A.min))
+        V.tensor_tensor(T.c[:], T.sa[:], T.f[:], A.mult).then_inc(sem.reb, 1)
+        for i in range(R):
+            V.tensor_tensor(p(i), p(i), T.f[:], A.mult).then_inc(sem.reb, 1)
+        V.wait_ge(sem.reb, R + 1)
+
+        V.wait_ge(sem.arrs, n_in)
+        s = done(V.tensor_tensor(T.c[:], T.c[:], T.sb[:], A.add))
         V.wait_ge(s, 1)
-        s = done(V.tensor_tensor(T.d[:], T.d[:], m_a, A.subtract))
-        S.wait_ge(s, 1)
-        s = done(S.activation(T.e[:], T.d[:], Exp))
-        V.wait_ge(s, 1)
-        s = done(V.tensor_tensor(T.e[:], T.e[:], s_b, A.mult))
-        V.wait_ge(s, 1)
-        s = done(V.tensor_tensor(T.e[:], T.e[:], s_a, A.add))
-        V.wait_ge(s, 1)
-        s = done(V.reciprocal(T.r[:], T.e[:]))
+        s = done(V.reciprocal(T.r[:], T.c[:]))
         V.wait_ge(s, 1)
         for i in range(1, R):
             V.tensor_tensor(blk(T.yb, i), p(i), T.r[:], A.mult).then_inc(sem.out, 1)

@@ -7,63 +7,49 @@ BANK = 512
 
 SCRATCH = {
     "xs": ("sbuf", [P, C], "float32"),
+    "h": ("sbuf", [P, C], "bfloat16"),
+    "z0": ("sbuf", [P, C], "float32"),
+    "q": ("psum", [P, BANK], "float32"),
     "land": ("sbuf", [P, 2 * C], "float32"),
-    "h": ("sbuf", [P, C // 4], "bfloat16"),
-    "q": ("sbuf", [P, C // 4], "float32"),
     "ta": ("sbuf", [P, C // 2], "float32"),
     "t2": ("sbuf", [P, C // 2], "float32"),
     "tb": ("psum", [P, BANK], "float32"),
     "z": ("sbuf", [P, 2 * C], "float32"),
-    "pa": ("psum", [P, BANK], "float32"),
-    "pb": ("psum", [P, BANK], "float32"),
-    "ma": ("sbuf", [P, C // 4], "bfloat16"),
+    "pp": ("sbuf", [P, 2 * C], "bfloat16"),
+    "ones": ("sbuf", [P, P], "bfloat16"),
+    "ident": ("sbuf", [P, P], "bfloat16"),
+    "ps": ("psum", [P, BANK], "float32"),
+    "p0": ("sbuf", [P, C // 4], "float32"),
     "sa": ("sbuf", [P, C // 4], "bfloat16"),
-    "mb": ("sbuf", [P, C // 4], "bfloat16"),
     "sb": ("sbuf", [P, C // 4], "bfloat16"),
+    "mf": ("sbuf", [P, C], "float32"),
+    "mb": ("sbuf", [P, C // 4], "float32"),
     "d": ("sbuf", [P, C // 4], "float32"),
     "f": ("sbuf", [P, C // 4], "float32"),
     "c": ("sbuf", [P, C // 4], "float32"),
     "r": ("sbuf", [P, C // 4], "float32"),
-    "yb": ("sbuf", [P, 2 * C], "bfloat16"),
+    "dr": ("sbuf", [P, C], "float32"),
+    "er": ("sbuf", [P, C], "float32"),
+    "n": ("psum", [P, BANK], "float32"),
+    "wl": ("sbuf", [P, C], "bfloat16"),
     "yl": ("sbuf", [P, C], "bfloat16"),
 }
-SEMAPHORES = ["ld", "ob", "sent", "arr1", "arrm", "arrs", "arr3", "st", "sub0", "sub1", "sub2", "sub3", "reb", "out"] + \
-             ["c%d" % i for i in range(1, 27)]
+SEMAPHORES = ["lda", "ldb", "sent", "arr1", "arrm", "arrs", "arra", "arrf", "arr3", "st",
+              "sub0", "sub1", "sub2", "sub3", "fill", "idn", "pe"] + ["c%d" % i for i in range(1, 33)]
 
 
 def _engines(mask):
     return [b for b in range(mask.bit_length()) if (mask >> b) & 1]
 
 
-def _shares(n, d):
-    s = 1
-    while 2 * s * d <= n:
-        s *= 2
-    out = [s] * d
-    left = n - s * d
-    for i in range(d):
-        if out[i] <= left:
-            left -= out[i]
-            out[i] *= 2
-    return out
-
-
-def _fan(topo, src, dsts):
-    m = topo.mask(src, dsts[0])
-    for t in dsts:
-        m &= topo.mask(src, t)
-    eng = _engines(m)
-    res, at = {}, 0
-    for t, n in zip(dsts, _shares(len(eng), len(dsts))):
-        res[t] = (sum(1 << b for b in eng[at:at + n]), n)
-        at += n
-    return res
+def _bits(eng):
+    return sum(1 << b for b in eng)
 
 
 def rank_program(g, core, T, topo):
     if T.rank_of(core) is None:
         return
-    V, S, Y, sem, A = g.vector, g.scalar, g.sync, T.sem, AluOpType
+    V, S, Y, E, sem, A = g.vector, g.scalar, g.sync, g.tensor, T.sem, AluOpType
     Exp = ActivationFunctionType.Exp
 
     def chip_of(c):
@@ -78,6 +64,8 @@ def rank_program(g, core, T, topo):
     own, far = gates(here, there), gates(there, here)
     K, R = len(own), len(here)
     W = C // K
+    aide = dict(zip(own, sorted([c for c in here if c not in own], key=lambda c: (topo.die(c), c))))
+    lord = {a: o for o, a in aide.items()}
 
     def blk(t, i, n=1):
         return t[:, i * W:(i + n) * W]
@@ -89,8 +77,17 @@ def rank_program(g, core, T, topo):
         rid, pid = topo.addr(t, core)
         return DstId(rid=rid, pnc=pid)
 
-    scatter = {c: _fan(topo, c, [o for o in own if o != c]) for c in here}
-    gather = {o: _fan(topo, o, [c for c in here if c != o]) for o in own}
+    def lanes(c):
+        eng = _engines(topo.mask(c, [t for t in here if t != c][0]))
+        main = _engines(topo.mask(c, far[own.index(c)])) if c in own else eng[:len(eng) // 2]
+        return eng, main, [b for b in eng if b not in main]
+
+    def hop1(c):
+        eng, main, rest = lanes(c)
+        to = [o for o in own if o != c]
+        return [(o, main) for o in to[:-1]] + [(to[-1], rest[:len(rest) // 2])]
+
+    eng, main, rest = lanes(core)
     sent = 0
     count = [0]
 
@@ -100,16 +97,29 @@ def rank_program(g, core, T, topo):
         instr.then_inc(s, 1)
         return s
 
-    Y.dma_start(T.xs[:], T.x[:]).then_inc(sem.ld, 16)
+    H = C // 2
+    Y.dma_start(T.xs[:, 0:H], T.x[:, 0:H]).then_inc(sem.lda, 16)
+    S.dma_start(T.xs[:, H:C], T.x[:, H:C]).then_inc(sem.ldb, 16)
     if core in own:
-        S.dma_start(blk(T.land, 0), blk(T.x, own.index(core))).then_inc(sem.ob, 16)
+        V.memset(T.ones[:], 1.0).then_inc(sem.fill, 1)
 
-    g.wait_ge(sem.ld, 16)
-    g.remote_dma_fused(
-        [RemoteDMATransfer(dst_ids=[dst(o)], dma_engine_mask=m, remote_sem=sem.arr1,
-                           src=blk(T.xs, own.index(o)), dst=blk(T.land, slot(o, core)))
-         for o, (m, n) in scatter[core].items()], local_sem=sem.sent)
-    sent += sum(n for m, n in scatter[core].values())
+    seen = []
+    for o, e in hop1(core):
+        part = sem.lda if (own.index(o) + 1) * W <= H else sem.ldb
+        if part not in seen:
+            seen.append(part)
+            g.wait_ge(part, 16)
+        rid, pid = topo.addr(o, core)
+        g.remote_dma(blk(T.land, slot(o, core)), blk(T.xs, own.index(o)), sem.arr1, sem.sent, pid, rid, _bits(e))
+        sent += len(e)
+
+    V.wait_ge(sem.lda, 16)
+    V.wait_ge(sem.ldb, 16)
+    s = done(V.tensor_copy(T.h[:], T.xs[:]))
+    V.wait_ge(s, 1)
+    s = done(V.tensor_tensor(T.z0[:], T.xs[:], T.h[:], A.subtract))
+    S.wait_ge(s, 1)
+    sq = done(S.activation(T.q[:, 0:C], T.z0[:], Exp))
 
     if core in own:
         k = own.index(core)
@@ -117,92 +127,110 @@ def rank_program(g, core, T, topo):
         rid, pid = topo.addr(partner, core)
         mk = topo.mask(core, partner)
         n_out, n_in = len(_engines(mk)), len(_engines(topo.mask(partner, core)))
+        mine = blk(T.mf, k)
 
-        def p(i):
-            return blk(T.z, i) if i < 4 else blk(T.pa, i - 4) if i < 6 else blk(T.pb, i - 6)
+        sl = done(V.tensor_copy(blk(T.land, 0), blk(T.h, k)))
+        g.wait_ge(sem.fill, 1)
+        g.affine_select(T.ident[:], T.ones[:], [[-1, P]], A.is_equal, 0.0, 0, 1).then_inc(sem.idn, 1)
 
-        V.wait_ge(sem.ob, 16)
-        s = done(V.tensor_copy(T.h[:], blk(T.land, 0)))
-        V.wait_ge(s, 1)
-        s = done(V.tensor_tensor(T.q[:], blk(T.land, 0), T.h[:], A.subtract))
-        S.wait_ge(s, 1)
-        sq = done(S.activation(T.q[:], T.q[:], Exp))
-
-        V.wait_ge(sem.arr1, sum(scatter[c][core][1] for c in here if c != core))
+        V.wait_ge(sl, 1)
+        V.wait_ge(sem.arr1, sum(len(e) for c in here if c != core for o, e in hop1(c) if o == core))
         s1 = done(V.tensor_tensor(T.ta[:], blk(T.land, 0, 2), blk(T.land, 4, 2), A.max))
         s2 = done(V.tensor_tensor(blk(T.tb, 0, 2), blk(T.land, 2, 2), blk(T.land, 6, 2), A.max))
         V.wait_ge(s1, 1)
         V.wait_ge(s2, 1)
         s = done(V.tensor_tensor(T.t2[:], T.ta[:], blk(T.tb, 0, 2), A.max))
         V.wait_ge(s, 1)
-        sm = done(V.tensor_tensor(T.ma[:], blk(T.t2, 0), blk(T.t2, 1), A.max))
+        sm = done(V.tensor_tensor(mine, blk(T.t2, 0), blk(T.t2, 1), A.max))
+        sm1 = done(V.tensor_tensor(blk(T.tb, 2), blk(T.t2, 0), blk(T.t2, 1), A.max))
+        sm2 = done(V.tensor_tensor(blk(T.tb, 3), blk(T.t2, 0), blk(T.t2, 1), A.max))
 
         g.wait_ge(sm, 1)
-        g.remote_dma(T.mb[:], T.ma[:], sem.arrm, sem.sent, pid, rid, mk)
+        g.remote_dma(T.mb[:], mine, sem.arrm, sem.sent, pid, rid, mk)
         sent += n_out
+        arid, apid = topo.addr(aide[core], core)
+        g.remote_dma(mine, mine, sem.arra, sem.sent, apid, arid, _bits(rest))
+        sent += len(rest)
 
         V.wait_ge(sm, 1)
-        V.tensor_tensor(blk(T.z, 0), T.h[:], T.ma[:], A.subtract).then_inc(sem.sub0, 1)
-        for i in range(1, R):
-            V.tensor_tensor(blk(T.z, i), blk(T.land, i), T.ma[:], A.subtract).then_inc(
-                sem.sub1 if i < 4 else sem.sub2 if i < 6 else sem.sub3, 1)
-        S.wait_ge(sem.sub0, 1)
-        e0 = done(S.activation(blk(T.z, 0), blk(T.z, 0), Exp))
-        S.wait_ge(sem.sub1, 3)
-        e1 = done(S.activation(blk(T.z, 1, 3), blk(T.z, 1, 3), Exp))
-        S.wait_ge(sem.sub2, 2)
-        e2 = done(S.activation(blk(T.pa, 0, 2), blk(T.z, 4, 2), Exp))
-        S.wait_ge(sem.sub3, 2)
-        e3 = done(S.activation(blk(T.pb, 0, 2), blk(T.z, 6, 2), Exp))
+        for i in range(2):
+            V.tensor_tensor(blk(T.z, i), blk(T.land, i), mine, A.subtract).then_inc(sem.sub0, 1)
+        V.wait_ge(sm1, 1)
+        V.wait_ge(sm2, 1)
+        for i in range(1, R // 2):
+            V.tensor_tensor(blk(T.z, 2 * i, 2), blk(T.land, 2 * i, 2), blk(T.tb, 2, 2), A.subtract).then_inc(
+                sem["sub%d" % i], 1)
+        ex = []
+        for i in range(R // 2):
+            S.wait_ge(sem["sub%d" % i], 2 if i == 0 else 1)
+            ex.append(done(S.activation(blk(T.pp, 2 * i, 2), blk(T.z, 2 * i, 2), Exp)))
+        E.wait_ge(sem.idn, 1)
+        for j in range(1, R):
+            if j == 1 or j % 2 == 0:
+                E.wait_ge(ex[j // 2], 1)
+            mmul = E.matmul(T.ps[:, 0:W], T.ident[:], blk(T.pp, j), j == 1, j == R - 1)
+        mmul.then_inc(sem.pe, 1)
         V.wait_ge(sq, 1)
-        V.wait_ge(e0, 1)
-        s = done(V.tensor_tensor(blk(T.z, 0), blk(T.z, 0), T.q[:], A.mult))
+        V.wait_ge(ex[0], 1)
+        s = done(V.tensor_tensor(T.p0[:], blk(T.pp, 0), blk(T.q, k), A.mult))
         V.wait_ge(s, 1)
-        V.wait_ge(e1, 1)
-        V.wait_ge(e2, 1)
-        s1 = done(V.tensor_tensor(T.ta[:], blk(T.z, 0, 2), blk(T.pa, 0, 2), A.add))
-        V.wait_ge(e3, 1)
-        s2 = done(V.tensor_tensor(blk(T.tb, 2, 2), blk(T.z, 2, 2), blk(T.pb, 0, 2), A.add))
-        V.wait_ge(s1, 1)
-        V.wait_ge(s2, 1)
-        s = done(V.tensor_tensor(T.t2[:], T.ta[:], blk(T.tb, 2, 2), A.add))
-        V.wait_ge(s, 1)
-        ss = done(V.tensor_tensor(T.sa[:], blk(T.t2, 0), blk(T.t2, 1), A.add))
+        V.wait_ge(sem.pe, 1)
+        ss = done(V.tensor_tensor(T.sa[:], T.p0[:], T.ps[:, 0:W], A.add))
 
         g.wait_ge(ss, 1)
         g.remote_dma(T.sb[:], T.sa[:], sem.arrs, sem.sent, pid, rid, mk)
         sent += n_out
 
         V.wait_ge(sem.arrm, n_in)
-        s = done(V.tensor_tensor(T.d[:], T.mb[:], T.ma[:], A.subtract))
+        s = done(V.tensor_tensor(T.d[:], T.mb[:], mine, A.subtract))
         V.wait_ge(s, 1)
         s = done(V.tensor_scalar(T.d[:], T.d[:], CLAMP, -CLAMP, A.min, A.max))
         S.wait_ge(s, 1)
         s = done(S.activation(T.f[:], T.d[:], Exp, scale=-1.0))
         V.wait_ge(s, 1)
         V.wait_ge(ss, 1)
-        V.tensor_tensor(T.c[:], T.sa[:], T.f[:], A.mult).then_inc(sem.reb, 1)
-        for i in range(R):
-            V.tensor_tensor(p(i), p(i), T.f[:], A.mult).then_inc(sem.reb, 1)
-        V.wait_ge(sem.reb, R + 1)
+        s = done(V.tensor_tensor(T.c[:], T.sa[:], T.f[:], A.mult))
+        V.wait_ge(s, 1)
 
         V.wait_ge(sem.arrs, n_in)
         s = done(V.tensor_tensor(T.c[:], T.c[:], T.sb[:], A.add))
         V.wait_ge(s, 1)
         s = done(V.reciprocal(T.r[:], T.c[:]))
         V.wait_ge(s, 1)
-        for i in range(1, R):
-            V.tensor_tensor(blk(T.yb, i), p(i), T.r[:], A.mult).then_inc(sem.out, 1)
-        V.tensor_tensor(blk(T.yl, k), p(0), T.r[:], A.mult).then_inc(sem.arr3, 1)
+        sw = done(V.tensor_tensor(blk(T.wl, k), T.f[:], T.r[:], A.mult))
 
-        g.wait_ge(sem.out, R - 1)
+        to = [c for c in here if c != core]
+        g.wait_ge(sw, 1)
         g.remote_dma_fused(
-            [RemoteDMATransfer(dst_ids=[dst(c)], dma_engine_mask=m, remote_sem=sem.arr3,
-                               src=blk(T.yb, slot(core, c)), dst=blk(T.yl, k))
-             for c, (m, n) in gather[core].items()], local_sem=sem.sent)
-        sent += sum(n for m, n in gather[core].values())
+            [RemoteDMATransfer(dst_ids=[dst(c) for c in to], dma_engine_mask=_bits(eng), remote_sem=sem.arr3,
+                               srcs=[blk(T.wl, k)], dsts=[blk(T.wl, k) for c in to])], local_sem=sem.sent)
+        sent += len(eng)
+        V.wait_ge(sw, 1)
 
-    Y.wait_ge(sem.arr3, sum(gather[o][core][1] for o in own if o != core) + (1 if core in own else 0))
+    if core in lord:
+        o = lord[core]
+        k = own.index(o)
+        n_a = len(lanes(o)[2])
+        to = [c for c in here if c != core and c != o]
+        g.wait_ge(sem.arra, n_a)
+        g.remote_dma_fused(
+            [RemoteDMATransfer(dst_ids=[dst(c) for c in to], dma_engine_mask=_bits(eng), remote_sem=sem.arrf,
+                               srcs=[blk(T.mf, k)], dsts=[blk(T.mf, k) for c in to])], local_sem=sem.sent)
+        sent += len(eng)
+        V.wait_ge(sem.arra, n_a)
+
+    V.wait_ge(sem.arrf, sum(len(lanes(a)[0]) for o, a in aide.items() if core != o and core != a))
+    s = done(V.tensor_tensor(T.dr[:], T.h[:], T.mf[:], A.subtract))
+    S.wait_ge(s, 1)
+    s = done(S.activation(T.er[:], T.dr[:], Exp))
+    V.wait_ge(s, 1)
+    V.wait_ge(sq, 1)
+    s = done(V.tensor_tensor(T.n[:, 0:C], T.er[:], T.q[:, 0:C], A.mult))
+    V.wait_ge(s, 1)
+
+    V.wait_ge(sem.arr3, sum(len(lanes(o)[0]) for o in own if o != core))
+    s = done(V.tensor_tensor(T.yl[:], T.n[:, 0:C], T.wl[:], A.mult))
+    Y.wait_ge(s, 1)
     Y.dma_start(T.y[:], T.yl[:]).then_inc(sem.st, 16)
     g.wait_ge(sem.sent, sent)
     g.wait_ge(sem.st, 16)

from concourse.bass import DstId, RemoteDMATransfer
from concourse.mybir import AluOpType, ActivationFunctionType

P, C = 128, 128
CLAMP = 60.0
BANK = 512

SCRATCH = {
    "xs": ("sbuf", [P, C], "float32"),
    "h": ("sbuf", [P, C], "bfloat16"),
    "z0": ("sbuf", [P, C], "float32"),
    "q": ("psum", [P, BANK], "float32"),
    "land": ("sbuf", [P, 2 * C], "float32"),
    "ta": ("sbuf", [P, C // 2], "float32"),
    "t2": ("sbuf", [P, C // 2], "float32"),
    "tb": ("psum", [P, BANK], "float32"),
    "z": ("sbuf", [P, 2 * C], "float32"),
    "pp": ("sbuf", [P, 2 * C], "bfloat16"),
    "ones": ("sbuf", [P, P], "bfloat16"),
    "ident": ("sbuf", [P, P], "bfloat16"),
    "ps": ("psum", [P, BANK], "float32"),
    "p0": ("sbuf", [P, C // 4], "float32"),
    "sa": ("sbuf", [P, C // 4], "bfloat16"),
    "sb": ("sbuf", [P, C // 4], "bfloat16"),
    "mf": ("sbuf", [P, C], "float32"),
    "mb": ("sbuf", [P, C // 4], "float32"),
    "d": ("sbuf", [P, C // 4], "float32"),
    "f": ("sbuf", [P, C // 4], "float32"),
    "c": ("sbuf", [P, C // 4], "float32"),
    "r": ("sbuf", [P, C // 4], "float32"),
    "dr": ("sbuf", [P, C], "float32"),
    "er": ("sbuf", [P, C], "float32"),
    "n": ("psum", [P, BANK], "float32"),
    "wl": ("sbuf", [P, C], "bfloat16"),
    "yl": ("sbuf", [P, C], "bfloat16"),
}
SEMAPHORES = ["lda", "ldb", "sent", "arr1", "arrm", "arrs", "arra", "arrf", "arr3", "st",
              "sub0", "sub1", "sub2", "sub3", "fill", "idn", "pe"] + ["c%d" % i for i in range(1, 33)]


def _engines(mask):
    return [b for b in range(mask.bit_length()) if (mask >> b) & 1]


def _bits(eng):
    return sum(1 << b for b in eng)


def rank_program(g, core, T, topo):
    if T.rank_of(core) is None:
        return
    V, S, Y, E, sem, A = g.vector, g.scalar, g.sync, g.tensor, T.sem, AluOpType
    Exp = ActivationFunctionType.Exp

    def chip_of(c):
        return (topo.host(c), topo.chip(c))

    here = [c for c in T.cores if chip_of(c) == chip_of(core)]
    there = [c for c in T.cores if chip_of(c) != chip_of(core)]

    def gates(a, b):
        return sorted([c for c in a if all(topo.may_write(c, t) for t in b)], key=lambda c: (topo.die(c), c))

    own, far = gates(here, there), gates(there, here)
    K, R = len(own), len(here)
    W = C // K
    aide = dict(zip(own, sorted([c for c in here if c not in own], key=lambda c: (topo.die(c), c))))
    lord = {a: o for o, a in aide.items()}

    def blk(t, i, n=1):
        return t[:, i * W:(i + n) * W]

    def slot(o, c):
        return 0 if c == o else 1 + [x for x in here if x != o].index(c)

    def dst(t):
        rid, pid = topo.addr(t, core)
        return DstId(rid=rid, pnc=pid)

    def lanes(c):
        eng = _engines(topo.mask(c, [t for t in here if t != c][0]))
        main = _engines(topo.mask(c, far[own.index(c)])) if c in own else eng[:len(eng) // 2]
        return eng, main, [b for b in eng if b not in main]

    def hop1(c):
        eng, main, rest = lanes(c)
        to = [o for o in own if o != c]
        return [(o, main) for o in to[:-1]] + [(to[-1], rest[:len(rest) // 2])]

    eng, main, rest = lanes(core)
    sent = 0
    count = [0]

    def done(instr):
        count[0] += 1
        s = sem["c%d" % count[0]]
        instr.then_inc(s, 1)
        return s

    H = C // 2
    Y.dma_start(T.xs[:, 0:H], T.x[:, 0:H]).then_inc(sem.lda, 16)
    S.dma_start(T.xs[:, H:C], T.x[:, H:C]).then_inc(sem.ldb, 16)
    if core in own:
        V.memset(T.ones[:], 1.0).then_inc(sem.fill, 1)

    seen = []
    for o, e in hop1(core):
        part = sem.lda if (own.index(o) + 1) * W <= H else sem.ldb
        if part not in seen:
            seen.append(part)
            g.wait_ge(part, 16)
        rid, pid = topo.addr(o, core)
        g.remote_dma(blk(T.land, slot(o, core)), blk(T.xs, own.index(o)), sem.arr1, sem.sent, pid, rid, _bits(e))
        sent += len(e)

    V.wait_ge(sem.lda, 16)
    V.wait_ge(sem.ldb, 16)
    s = done(V.tensor_copy(T.h[:], T.xs[:]))
    V.wait_ge(s, 1)
    s = done(V.tensor_tensor(T.z0[:], T.xs[:], T.h[:], A.subtract))
    S.wait_ge(s, 1)
    sq = done(S.activation(T.q[:, 0:C], T.z0[:], Exp))

    if core in own:
        k = own.index(core)
        partner = far[k]
        rid, pid = topo.addr(partner, core)
        mk = topo.mask(core, partner)
        n_out, n_in = len(_engines(mk)), len(_engines(topo.mask(partner, core)))
        mine = blk(T.mf, k)

        sl = done(V.tensor_copy(blk(T.land, 0), blk(T.h, k)))
        g.wait_ge(sem.fill, 1)
        g.affine_select(T.ident[:], T.ones[:], [[-1, P]], A.is_equal, 0.0, 0, 1).then_inc(sem.idn, 1)

        V.wait_ge(sl, 1)
        V.wait_ge(sem.arr1, sum(len(e) for c in here if c != core for o, e in hop1(c) if o == core))
        s1 = done(V.tensor_tensor(T.ta[:], blk(T.land, 0, 2), blk(T.land, 4, 2), A.max))
        s2 = done(V.tensor_tensor(blk(T.tb, 0, 2), blk(T.land, 2, 2), blk(T.land, 6, 2), A.max))
        V.wait_ge(s1, 1)
        V.wait_ge(s2, 1)
        s = done(V.tensor_tensor(T.t2[:], T.ta[:], blk(T.tb, 0, 2), A.max))
        V.wait_ge(s, 1)
        sm = done(V.tensor_tensor(mine, blk(T.t2, 0), blk(T.t2, 1), A.max))
        sm1 = done(V.tensor_tensor(blk(T.tb, 2), blk(T.t2, 0), blk(T.t2, 1), A.max))
        sm2 = done(V.tensor_tensor(blk(T.tb, 3), blk(T.t2, 0), blk(T.t2, 1), A.max))

        g.wait_ge(sm, 1)
        g.remote_dma(T.mb[:], mine, sem.arrm, sem.sent, pid, rid, mk)
        sent += n_out
        arid, apid = topo.addr(aide[core], core)
        g.remote_dma(mine, mine, sem.arra, sem.sent, apid, arid, _bits(rest))
        sent += len(rest)

        V.wait_ge(sm, 1)
        for i in range(2):
            V.tensor_tensor(blk(T.z, i), blk(T.land, i), mine, A.subtract).then_inc(sem.sub0, 1)
        V.wait_ge(sm1, 1)
        V.wait_ge(sm2, 1)
        for i in range(1, R // 2):
            V.tensor_tensor(blk(T.z, 2 * i, 2), blk(T.land, 2 * i, 2), blk(T.tb, 2, 2), A.subtract).then_inc(
                sem["sub%d" % i], 1)
        ex = []
        for i in range(R // 2):
            S.wait_ge(sem["sub%d" % i], 2 if i == 0 else 1)
            ex.append(done(S.activation(blk(T.pp, 2 * i, 2), blk(T.z, 2 * i, 2), Exp)))
        E.wait_ge(sem.idn, 1)
        for j in range(1, R):
            if j == 1 or j % 2 == 0:
                E.wait_ge(ex[j // 2], 1)
            mmul = E.matmul(T.ps[:, 0:W], T.ident[:], blk(T.pp, j), j == 1, j == R - 1)
        mmul.then_inc(sem.pe, 1)
        V.wait_ge(sq, 1)
        V.wait_ge(ex[0], 1)
        s = done(V.tensor_tensor(T.p0[:], blk(T.pp, 0), blk(T.q, k), A.mult))
        V.wait_ge(s, 1)
        V.wait_ge(sem.pe, 1)
        ss = done(V.tensor_tensor(T.sa[:], T.p0[:], T.ps[:, 0:W], A.add))

        g.wait_ge(ss, 1)
        g.remote_dma(T.sb[:], T.sa[:], sem.arrs, sem.sent, pid, rid, mk)
        sent += n_out

        V.wait_ge(sem.arrm, n_in)
        s = done(V.tensor_tensor(T.d[:], T.mb[:], mine, A.subtract))
        V.wait_ge(s, 1)
        s = done(V.tensor_scalar(T.d[:], T.d[:], CLAMP, -CLAMP, A.min, A.max))
        S.wait_ge(s, 1)
        s = done(S.activation(T.f[:], T.d[:], Exp, scale=-1.0))
        V.wait_ge(s, 1)
        V.wait_ge(ss, 1)
        s = done(V.tensor_tensor(T.c[:], T.sa[:], T.f[:], A.mult))
        V.wait_ge(s, 1)

        V.wait_ge(sem.arrs, n_in)
        s = done(V.tensor_tensor(T.c[:], T.c[:], T.sb[:], A.add))
        V.wait_ge(s, 1)
        s = done(V.reciprocal(T.r[:], T.c[:]))
        V.wait_ge(s, 1)
        sw = done(V.tensor_tensor(blk(T.wl, k), T.f[:], T.r[:], A.mult))

        to = [c for c in here if c != core]
        g.wait_ge(sw, 1)
        g.remote_dma_fused(
            [RemoteDMATransfer(dst_ids=[dst(c) for c in to], dma_engine_mask=_bits(eng), remote_sem=sem.arr3,
                               srcs=[blk(T.wl, k)], dsts=[blk(T.wl, k) for c in to])], local_sem=sem.sent)
        sent += len(eng)
        V.wait_ge(sw, 1)

    if core in lord:
        o = lord[core]
        k = own.index(o)
        n_a = len(lanes(o)[2])
        to = [c for c in here if c != core and c != o]
        g.wait_ge(sem.arra, n_a)
        g.remote_dma_fused(
            [RemoteDMATransfer(dst_ids=[dst(c) for c in to], dma_engine_mask=_bits(eng), remote_sem=sem.arrf,
                               srcs=[blk(T.mf, k)], dsts=[blk(T.mf, k) for c in to])], local_sem=sem.sent)
        sent += len(eng)
        V.wait_ge(sem.arra, n_a)

    V.wait_ge(sem.arrf, sum(len(lanes(a)[0]) for o, a in aide.items() if core != o and core != a))
    s = done(V.tensor_tensor(T.dr[:], T.h[:], T.mf[:], A.subtract))
    S.wait_ge(s, 1)
    s = done(S.activation(T.er[:], T.dr[:], Exp))
    V.wait_ge(s, 1)
    V.wait_ge(sq, 1)
    s = done(V.tensor_tensor(T.n[:, 0:C], T.er[:], T.q[:, 0:C], A.mult))
    V.wait_ge(s, 1)

    V.wait_ge(sem.arr3, sum(len(lanes(o)[0]) for o in own if o != core))
    s = done(V.tensor_tensor(T.yl[:], T.n[:, 0:C], T.wl[:], A.mult))
    Y.wait_ge(s, 1)
    Y.dma_start(T.y[:], T.yl[:]).then_inc(sem.st, 16)
    g.wait_ge(sem.sent, sent)
    g.wait_ge(sem.st, 16)
